import numpy as np
import ml_dtypes

BF16 = ml_dtypes.bfloat16


def bf(x):
    return np.asarray(x, np.float32).astype(BF16)


def f32(x):
    return np.asarray(x, np.float32)


def f64(x):
    return np.asarray(x).astype(np.float64)


def striped(idx):
    return np.concatenate([l.reshape(-1, 16).T for l in idx])


def rows(idx, k):
    return np.tile(np.repeat(idx, 16, axis=0), (k // (16 * 8), 1))


def look(tab, idx):
    return np.take_along_axis(f64(tab), rows(idx, len(tab)), axis=1)


K, S, V, N, M = 256, 2048, 2048, 2048, 512


def setup_inputs():
    return {"tab": f32(np.random.standard_normal((2, K, S))), "y": f32(np.random.standard_normal((K, V))), "w": bf(np.random.standard_normal((K, M)) / np.sqrt(K)), "b": f32(0.5 * np.random.standard_normal((M, 1))), "offs": striped(np.stack([np.random.permutation(S)[:N] for _ in range(8)]))}


def reference(tab, y, w, b, offs):
    idx = np.stack([g.T.reshape(-1) for g in np.split(offs, 8)])
    x = (look(tab[0], idx) * f64(y)) * (np.maximum(look(tab[1], idx), 0.0))
    return np.maximum(f64(w).T @ x + f64(b), 0.0)

@@ -1,0 +1,58 @@
+import concourse.mybir as mybir
+
+P = 128
+PIECE = 512
+LANES = 16
+
+FLOPS = 2 * 256 * 512 * 2048
+
+F32, BF16, U16 = mybir.dt.float32, mybir.dt.bfloat16, mybir.dt.uint16
+MULT = mybir.AluOpType.mult
+RELU = mybir.ActivationFunctionType.Relu
+
+
+def tile_lookup_vg_mulrelu_relu_kernel(tc, tab, y, w, b, offs, out):
+    nc = tc.nc
+    rows, places = tab.shape[1], tab.shape[2]
+    entries = y.shape[1]
+    blocks, pieces, groups = rows // P, entries // PIECE, w.shape[1] // P
+    out_rows = out.rearrange("(p k) n -> p k n", k=groups)
+
+    with (
+        tc.tile_pool(name="held", bufs=1) as held,
+        tc.psum_pool(name="psum", bufs=8) as psum,
+    ):
+        offsets = held.tile([P, entries // LANES], U16, name="offsets")
+        nc.sync.dma_start(offsets[:], offs)
+        bias = held.tile([P, groups], F32, name="bias")
+        nc.sync.dma_start(bias[:], b.rearrange("(p k) o -> p (k o)", k=groups))
+        weights = held.tile([P, blocks, groups * P], BF16, name="weights")
+        nc.sync.dma_start(weights[:], w.rearrange("(r p) m -> p r m", p=P))
+
+        x = {}
+        for r in range(blocks):
+            block = slice(r * P, (r + 1) * P)
+            gates = held.tile([P, places], F32, name=f"gates{r}")
+            nc.sync.dma_start(gates[:], tab[1, block, :])
+            values = held.tile([P, places], F32, name=f"values{r}")
+            nc.sync.dma_start(values[:], tab[0, block, :])
+            for c in range(pieces):
+                listed = offsets[:, c * PIECE // LANES : (c + 1) * PIECE // LANES]
+                stream = held.tile([P, PIECE], F32, name=f"stream{r}_{c}")
+                nc.sync.dma_start(stream[:], y[block, c * PIECE : (c + 1) * PIECE])
+                gate = held.tile([P, PIECE], F32, name=f"gate{r}_{c}")
+                nc.scalar.activation(gate[:], gates[:].indirect(listed), RELU)
+                scaled = held.tile([P, PIECE], F32, name=f"scaled{r}_{c}")
+                nc.vector.tensor_tensor(scaled[:], values[:].indirect(listed), stream[:], MULT)
+                x[r, c] = held.tile([P, PIECE], BF16, name=f"x{r}_{c}")
+                nc.vector.tensor_tensor(x[r, c][:], scaled[:], gate[:], MULT)
+
+        for c in range(pieces):
+            for k in range(groups):
+                acc = psum.tile([P, PIECE], F32, name="acc")
+                for r in range(blocks):
+                    nc.tensor.matmul(acc[:], weights[:, r, k::groups], x[r, c][:],
+                                     start=(r == 0), stop=(r == blocks - 1))
+                result = held.tile([P, PIECE], F32, name=f"result{c}_{k}")
+                nc.scalar.activation(result[:], acc[:], RELU, bias=bias[:, k : k + 1])
+                nc.sync.dma_start(out_rows[:, k, c * PIECE : (c + 1) * PIECE], result[:])

@@ -3,56 +3,83 @@ import concourse.mybir as mybir
 P = 128
 PIECE = 512
 LANES = 16
+AHEAD = 2
 
 FLOPS = 2 * 256 * 512 * 2048
 
 F32, BF16, U16 = mybir.dt.float32, mybir.dt.bfloat16, mybir.dt.uint16
-MULT = mybir.AluOpType.mult
+MULT, ADD, MAX = mybir.AluOpType.mult, mybir.AluOpType.add, mybir.AluOpType.max
 RELU = mybir.ActivationFunctionType.Relu
 
 
 def tile_lookup_vg_mulrelu_relu_kernel(tc, tab, y, w, b, offs, out):
     nc = tc.nc
     rows, places = tab.shape[1], tab.shape[2]
-    entries = y.shape[1]
-    blocks, pieces, groups = rows // P, entries // PIECE, w.shape[1] // P
+    blocks, pieces, groups = rows // P, y.shape[1] // PIECE, w.shape[1] // P
+    assert blocks == 2
     out_rows = out.rearrange("(p k) n -> p k n", k=groups)
 
     with (
         tc.tile_pool(name="held", bufs=1) as held,
         tc.psum_pool(name="psum", bufs=8) as psum,
     ):
-        offsets = held.tile([P, entries // LANES], U16, name="offsets")
-        nc.sync.dma_start(offsets[:], offs)
-        bias = held.tile([P, groups], F32, name="bias")
-        nc.sync.dma_start(bias[:], b.rearrange("(p k) o -> p (k o)", k=groups))
-        weights = held.tile([P, blocks, groups * P], BF16, name="weights")
-        nc.sync.dma_start(weights[:], w.rearrange("(r p) m -> p r m", p=P))
+        def load(name, source, dtype):
+            tile = held.tile(list(source.shape), dtype, name=name)
+            nc.sync.dma_start(tile[:], source)
+            return tile
 
-        x = {}
-        for r in range(blocks):
-            block = slice(r * P, (r + 1) * P)
-            gates = held.tile([P, places], F32, name=f"gates{r}")
-            nc.sync.dma_start(gates[:], tab[1, block, :])
-            values = held.tile([P, places], F32, name=f"values{r}")
-            nc.sync.dma_start(values[:], tab[0, block, :])
-            for c in range(pieces):
-                listed = offsets[:, c * PIECE // LANES : (c + 1) * PIECE // LANES]
-                stream = held.tile([P, PIECE], F32, name=f"stream{r}_{c}")
-                nc.sync.dma_start(stream[:], y[block, c * PIECE : (c + 1) * PIECE])
-                gate = held.tile([P, PIECE], F32, name=f"gate{r}_{c}")
-                nc.scalar.activation(gate[:], gates[:].indirect(listed), RELU)
-                scaled = held.tile([P, PIECE], F32, name=f"scaled{r}_{c}")
-                nc.vector.tensor_tensor(scaled[:], values[:].indirect(listed), stream[:], MULT)
-                x[r, c] = held.tile([P, PIECE], BF16, name=f"x{r}_{c}")
-                nc.vector.tensor_tensor(x[r, c][:], scaled[:], gate[:], MULT)
+        def load_table(which, r):
+            return load(f"table{which}_{r}", tab[which, r * P : (r + 1) * P, :], F32)
+
+        def load_stream(r, c):
+            return load(f"stream{r}_{c}", y[r * P : (r + 1) * P, c * PIECE : (c + 1) * PIECE], F32)
+
+        gates, values, stream = {}, {}, {}
+        offsets = load("offsets", offs, U16)
+        gates[0] = load_table(1, 0)
+        values[0] = load_table(0, 0)
+        for c in range(AHEAD):
+            stream[0, c] = load_stream(0, c)
+        gates[1] = load_table(1, 1)
+        weights = load("weights", w.rearrange("(r p) m -> p r m", p=P), BF16)
+        bias = load("bias", b.rearrange("(p k) o -> p (k o)", k=groups), F32)
+        stream[1, 0] = load_stream(1, 0)
+        values[1] = load_table(0, 1)
+        for c in range(1, pieces):
+            for r in range(blocks):
+                if (r, c) not in stream:
+                    stream[r, c] = load_stream(r, c)
+
+        def listed(c):
+            return offsets[:, c * PIECE // LANES : (c + 1) * PIECE // LANES]
+
+        def look_up_gate(r, c):
+            gate = held.tile([P, PIECE], F32, name=f"gate{r}_{c}")
+            nc.scalar.activation(gate[:], gates[r][:].indirect(listed(c)), RELU)
+            return gate
+
+        def look_up_x(r, c):
+            scaled = held.tile([P, PIECE], F32, name=f"scaled{r}_{c}")
+            nc.vector.tensor_tensor(scaled[:], values[r][:].indirect(listed(c)), stream[r, c][:], MULT)
+            gated = held.tile([P, PIECE], BF16, name=f"x{r}_{c}")
+            nc.vector.tensor_tensor(gated[:], scaled[:], gate[r, c][:], MULT)
+            return gated
+
+        gate = {(r, c): look_up_gate(r, c) for r in range(blocks) for c in range(pieces)}
+        x = {(0, c): look_up_x(0, c) for c in range(AHEAD)}
 
         for c in range(pieces):
+            for r in range(blocks):
+                if (r, c) not in x:
+                    x[r, c] = look_up_x(r, c)
             for k in range(groups):
                 acc = psum.tile([P, PIECE], F32, name="acc")
                 for r in range(blocks):
                     nc.tensor.matmul(acc[:], weights[:, r, k::groups], x[r, c][:],
                                      start=(r == 0), stop=(r == blocks - 1))
                 result = held.tile([P, PIECE], F32, name=f"result{c}_{k}")
-                nc.scalar.activation(result[:], acc[:], RELU, bias=bias[:, k : k + 1])
+                if c == pieces - 1 and k % 2 == 1:
+                    nc.vector.tensor_scalar(result[:], acc[:], bias[:, k : k + 1], 0.0, ADD, MAX)
+                else:
+                    nc.scalar.activation(result[:], acc[:], RELU, bias=bias[:, k : k + 1])
                 nc.sync.dma_start(out_rows[:, k, c * PIECE : (c + 1) * PIECE], result[:])

@@ -1,9 +1,10 @@
 import concourse.mybir as mybir
 
 P = 128
-PIECE = 512
 LANES = 16
-AHEAD = 2
+GATE_PIECE = 512
+WIDTHS = [256, 512, 512, 512, 256]
+AHEAD = 3
 
 FLOPS = 2 * 256 * 512 * 2048
 
@@ -14,9 +15,10 @@ RELU = mybir.ActivationFunctionType.Relu
 
 def tile_lookup_vg_mulrelu_relu_kernel(tc, tab, y, w, b, offs, out):
     nc = tc.nc
-    rows, places = tab.shape[1], tab.shape[2]
-    blocks, pieces, groups = rows // P, y.shape[1] // PIECE, w.shape[1] // P
-    assert blocks == 2
+    entries, groups = y.shape[1], w.shape[1] // P
+    assert tab.shape[1] == 2 * P and sum(WIDTHS) == entries
+    spans = [slice(sum(WIDTHS[:s]), sum(WIDTHS[: s + 1])) for s in range(len(WIDTHS))]
+    last = len(spans) - 1
     out_rows = out.rearrange("(p k) n -> p k n", k=groups)
 
     with (
@@ -28,58 +30,60 @@ def tile_lookup_vg_mulrelu_relu_kernel(tc, tab, y, w, b, offs, out):
             nc.sync.dma_start(tile[:], source)
             return tile
 
-        def load_table(which, r):
-            return load(f"table{which}_{r}", tab[which, r * P : (r + 1) * P, :], F32)
+        def block(r):
+            return slice(r * P, (r + 1) * P)
 
-        def load_stream(r, c):
-            return load(f"stream{r}_{c}", y[r * P : (r + 1) * P, c * PIECE : (c + 1) * PIECE], F32)
+        def load_stream(r, s):
+            return load(f"stream{r}_{s}", y[block(r), spans[s]], F32)
 
-        gates, values, stream = {}, {}, {}
+        gates, values, weights, stream = {}, {}, {}, {}
         offsets = load("offsets", offs, U16)
-        gates[0] = load_table(1, 0)
-        values[0] = load_table(0, 0)
-        for c in range(AHEAD):
-            stream[0, c] = load_stream(0, c)
-        gates[1] = load_table(1, 1)
-        weights = load("weights", w.rearrange("(r p) m -> p r m", p=P), BF16)
+        gates[0] = load("gates0", tab[1, block(0), :], F32)
+        values[0] = load("values0", tab[0, block(0), :], F32)
+        for s in range(2):
+            stream[0, s] = load_stream(0, s)
+        gates[1] = load("gates1", tab[1, block(1), :], F32)
+        for s in range(2, AHEAD):
+            stream[0, s] = load_stream(0, s)
+        weights[0] = load("weights0", w[block(0), :], BF16)
         bias = load("bias", b.rearrange("(p k) o -> p (k o)", k=groups), F32)
         stream[1, 0] = load_stream(1, 0)
-        values[1] = load_table(0, 1)
-        for c in range(1, pieces):
-            for r in range(blocks):
-                if (r, c) not in stream:
-                    stream[r, c] = load_stream(r, c)
+        values[1] = load("values1", tab[0, block(1), :], F32)
+        weights[1] = load("weights1", w[block(1), :], BF16)
+        for s in range(1, len(spans)):
+            for r in range(2):
+                if (r, s) not in stream:
+                    stream[r, s] = load_stream(r, s)
 
-        def listed(c):
-            return offsets[:, c * PIECE // LANES : (c + 1) * PIECE // LANES]
+        def listed(columns):
+            return offsets[:, columns.start // LANES : columns.stop // LANES]
 
-        def look_up_gate(r, c):
-            gate = held.tile([P, PIECE], F32, name=f"gate{r}_{c}")
-            nc.scalar.activation(gate[:], gates[r][:].indirect(listed(c)), RELU)
-            return gate
+        gate = {}
+        for r in range(2):
+            gate[r] = held.tile([P, entries], F32, name=f"gate{r}")
+            for start in range(0, entries, GATE_PIECE):
+                columns = slice(start, start + GATE_PIECE)
+                nc.scalar.activation(gate[r][:, columns], gates[r][:].indirect(listed(columns)), RELU)
 
-        def look_up_x(r, c):
-            scaled = held.tile([P, PIECE], F32, name=f"scaled{r}_{c}")
-            nc.vector.tensor_tensor(scaled[:], values[r][:].indirect(listed(c)), stream[r, c][:], MULT)
-            gated = held.tile([P, PIECE], BF16, name=f"x{r}_{c}")
-            nc.vector.tensor_tensor(gated[:], scaled[:], gate[r, c][:], MULT)
+        def look_up_x(r, s):
+            scaled = held.tile([P, WIDTHS[s]], F32, name=f"scaled{r}_{s}")
+            nc.vector.tensor_tensor(scaled[:], values[r][:].indirect(listed(spans[s])), stream[r, s][:], MULT)
+            gated = held.tile([P, WIDTHS[s]], BF16, name=f"x{r}_{s}")
+            nc.vector.tensor_tensor(gated[:], scaled[:], gate[r][:, spans[s]], MULT)
             return gated
 
-        gate = {(r, c): look_up_gate(r, c) for r in range(blocks) for c in range(pieces)}
-        x = {(0, c): look_up_x(0, c) for c in range(AHEAD)}
-
-        for c in range(pieces):
-            for r in range(blocks):
-                if (r, c) not in x:
-                    x[r, c] = look_up_x(r, c)
+        x = {(0, s): look_up_x(0, s) for s in range(AHEAD)}
+        for s, columns in enumerate(spans):
+            for r in range(2):
+                if (r, s) not in x:
+                    x[r, s] = look_up_x(r, s)
             for k in range(groups):
-                acc = psum.tile([P, PIECE], F32, name="acc")
-                for r in range(blocks):
-                    nc.tensor.matmul(acc[:], weights[:, r, k::groups], x[r, c][:],
-                                     start=(r == 0), stop=(r == blocks - 1))
-                result = held.tile([P, PIECE], F32, name=f"result{c}_{k}")
-                if c == pieces - 1 and k % 2 == 1:
+                acc = psum.tile([P, WIDTHS[s]], F32, name="acc")
+                for r in range(2):
+                    nc.tensor.matmul(acc[:], weights[r][:, k::groups], x[r, s][:], start=(r == 0), stop=(r == 1))
+                result = held.tile([P, WIDTHS[s]], F32, name=f"result{s}_{k}")
+                if s == last and k % 2 == 1:
                     nc.vector.tensor_scalar(result[:], acc[:], bias[:, k : k + 1], 0.0, ADD, MAX)
                 else:
                     nc.scalar.activation(result[:], acc[:], RELU, bias=bias[:, k : k + 1])
-                nc.sync.dma_start(out_rows[:, k, c * PIECE : (c + 1) * PIECE], result[:])
+                nc.sync.dma_start(out_rows[:, k, columns], result[:])

import concourse.mybir as mybir

P = 128
LANES = 16
GATE_PIECE = 512
WIDTHS = [256, 512, 512, 512, 256]
AHEAD = 3

FLOPS = 2 * 256 * 512 * 2048

F32, BF16, U16 = mybir.dt.float32, mybir.dt.bfloat16, mybir.dt.uint16
MULT, ADD, MAX = mybir.AluOpType.mult, mybir.AluOpType.add, mybir.AluOpType.max
RELU = mybir.ActivationFunctionType.Relu


def tile_lookup_vg_mulrelu_relu_kernel(tc, tab, y, w, b, offs, out):
    nc = tc.nc
    entries, groups = y.shape[1], w.shape[1] // P
    assert tab.shape[1] == 2 * P and sum(WIDTHS) == entries
    spans = [slice(sum(WIDTHS[:s]), sum(WIDTHS[: s + 1])) for s in range(len(WIDTHS))]
    last = len(spans) - 1
    out_rows = out.rearrange("(p k) n -> p k n", k=groups)

    with (
        tc.tile_pool(name="held", bufs=1) as held,
        tc.psum_pool(name="psum", bufs=8) as psum,
    ):
        def load(name, source, dtype):
            tile = held.tile(list(source.shape), dtype, name=name)
            nc.sync.dma_start(tile[:], source)
            return tile

        def block(r):
            return slice(r * P, (r + 1) * P)

        def load_stream(r, s):
            return load(f"stream{r}_{s}", y[block(r), spans[s]], F32)

        gates, values, weights, stream = {}, {}, {}, {}
        offsets = load("offsets", offs, U16)
        gates[0] = load("gates0", tab[1, block(0), :], F32)
        values[0] = load("values0", tab[0, block(0), :], F32)
        for s in range(2):
            stream[0, s] = load_stream(0, s)
        gates[1] = load("gates1", tab[1, block(1), :], F32)
        for s in range(2, AHEAD):
            stream[0, s] = load_stream(0, s)
        weights[0] = load("weights0", w[block(0), :], BF16)
        bias = load("bias", b.rearrange("(p k) o -> p (k o)", k=groups), F32)
        stream[1, 0] = load_stream(1, 0)
        values[1] = load("values1", tab[0, block(1), :], F32)
        weights[1] = load("weights1", w[block(1), :], BF16)
        for s in range(1, len(spans)):
            for r in range(2):
                if (r, s) not in stream:
                    stream[r, s] = load_stream(r, s)

        def listed(columns):
            return offsets[:, columns.start // LANES : columns.stop // LANES]

        gate = {}
        for r in range(2):
            gate[r] = held.tile([P, entries], F32, name=f"gate{r}")
            for start in range(0, entries, GATE_PIECE):
                columns = slice(start, start + GATE_PIECE)
                nc.scalar.activation(gate[r][:, columns], gates[r][:].indirect(listed(columns)), RELU)

        def look_up_x(r, s):
            scaled = held.tile([P, WIDTHS[s]], F32, name=f"scaled{r}_{s}")
            nc.vector.tensor_tensor(scaled[:], values[r][:].indirect(listed(spans[s])), stream[r, s][:], MULT)
            gated = held.tile([P, WIDTHS[s]], BF16, name=f"x{r}_{s}")
            nc.vector.tensor_tensor(gated[:], scaled[:], gate[r][:, spans[s]], MULT)
            return gated

        x = {(0, s): look_up_x(0, s) for s in range(AHEAD)}
        for s, columns in enumerate(spans):
            for r in range(2):
                if (r, s) not in x:
                    x[r, s] = look_up_x(r, s)
            for k in range(groups):
                acc = psum.tile([P, WIDTHS[s]], F32, name="acc")
                for r in range(2):
                    nc.tensor.matmul(acc[:], weights[r][:, k::groups], x[r, s][:], start=(r == 0), stop=(r == 1))
                result = held.tile([P, WIDTHS[s]], F32, name=f"result{s}_{k}")
                if s == last and k % 2 == 1:
                    nc.vector.tensor_scalar(result[:], acc[:], bias[:, k : k + 1], 0.0, ADD, MAX)
                else:
                    nc.scalar.activation(result[:], acc[:], RELU, bias=bias[:, k : k + 1])
                nc.sync.dma_start(out_rows[:, k, columns], result[:])
